import numpy as np
import ml_dtypes


def mxq(x, axis, fmt="e4m3"):
    dtype, down = {"e4m3": (ml_dtypes.float8_e4m3fn, 7), "e5m2": (ml_dtypes.float8_e5m2, 14)}[fmt]
    v = np.moveaxis(np.asarray(x, np.float32).astype(ml_dtypes.bfloat16).astype(np.float64), axis, -1)
    blocks = v.reshape(v.shape[:-1] + (-1, 32))
    amax = np.abs(blocks).max(-1, keepdims=True)
    byte = np.maximum(np.where(amax > 0, np.frexp(amax)[1] - 1 + 127, 0) - down, 1)
    scale = np.exp2(byte - 127.0)
    codes = (blocks / scale).astype(np.float32).astype(dtype).astype(np.float64)
    return np.moveaxis((codes * scale).reshape(v.shape), -1, axis)


WIDE = False


def mx_kscale(k):
    if not WIDE:
        return np.ones(k)
    levels = np.array([10, -10, 5, -5, 0])
    if k % 512:
        return np.exp2(np.random.permutation(np.resize(levels, k // 32))).repeat(32)
    a = np.empty((k // 512, 16))
    for p in range(k // 512):
        a[p, :8] = np.random.permutation(np.resize(levels, 8))
        for g in range(8):
            far = levels[np.abs(levels - a[p, g]) >= 10]
            a[p, g + 8] = far[np.random.randint(len(far))]
    return np.exp2(a.ravel()).repeat(32)


def f64(x):
    return np.asarray(x).astype(np.float64)


def striped(idx):
    return np.tile(idx.reshape(-1, 16).T, (8, 1)).astype(np.uint16)


def unstriped(offs):
    return offs[:16].T.reshape(-1).astype(np.int64)


E2M1 = np.array([0.0, 0.5, 1.0, 1.5, 2.0, 3.0, 4.0, 6.0, -0.0, -0.5, -1.0, -1.5, -2.0, -3.0, -4.0, -6.0])


def pack_weight(w, fmt):
    k, n = w.shape
    w = f64(np.asarray(w, np.float32).astype(ml_dtypes.bfloat16)).reshape(k // 32, 32, n)
    amax = np.abs(w).max(1)
    if fmt == "e4m3":
        byte = np.frexp(amax)[1] - 1 + 127 - 7
    else:
        mant, ex = np.frexp(amax / 6.0)
        byte = np.where(mant > 0.5, ex, ex - 1) + 127
    byte = np.clip(np.where(amax > 0, byte, 1), 1, 254)
    scaled = (w * np.exp2(127.0 - byte)[:, None, :]).reshape(k, n).astype(np.float32)
    by_word = np.ascontiguousarray(scaled.reshape(k // 512, 128, 4, n).transpose(0, 1, 3, 2))
    if fmt == "e4m3":
        words = by_word.astype(ml_dtypes.float8_e4m3fn).view(np.uint8)
    else:
        c = by_word.astype(ml_dtypes.float4_e2m1fn).view(np.uint8) & 0xF
        words = (c[..., 0::2] | (c[..., 1::2] << 4)).reshape(k // 512, 128, 2 * n)
    return np.ascontiguousarray(words), np.ascontiguousarray(byte.astype(np.uint8).reshape(k // 512, 16, n))


def unpack_weight(words, scales, fmt):
    g, _, n = scales.shape
    words = np.ascontiguousarray(words).reshape(g, 128, n, -1)
    if fmt == "e4m3":
        vals = words.view(ml_dtypes.float8_e4m3fn).astype(np.float64)
    else:
        nib = np.empty((g, 128, n, 4), np.uint8)
        nib[..., 0::2] = words & 0xF
        nib[..., 1::2] = words >> 4
        vals = E2M1[nib]
    vals = vals * np.repeat(np.exp2(scales.astype(np.float64) - 127.0), 8, axis=1)[..., None]
    return vals.transpose(0, 1, 3, 2).reshape(g * 512, n)


K, T, E, C, N = 1024, 640, 10, 128, 128
M = 512


def by_expert(wq, xq):
    return np.concatenate([wq[e].T @ xq[:, e * C:(e + 1) * C] for e in range(E)], axis=1)


def setup_inputs():
    n = np.random.standard_normal
    s = mx_kscale(K)[:, None]
    first = np.random.permutation(np.repeat(np.arange(E), T // E))
    second = (first + 1 + np.random.permutation(np.repeat(np.arange(E - 1), -(-T // (E - 1)))[:T])) % E
    while np.bincount(second, minlength=E).max() != T // E:
        load = np.bincount(second, minlength=E); hi, lo = int(load.argmax()), int(load.argmin())
        t = np.flatnonzero((second == hi) & (first != lo))[0]; second[t] = lo
    slot_token = np.empty(E * C, np.int64); pos = np.empty((2, T), np.int64); fill = np.zeros(E, np.int64)
    place = np.stack([np.random.permutation(C) for _ in range(E)])
    for r, deal in enumerate((first, second)):
        for t in np.random.permutation(T):
            e = deal[t]; j = e * C + place[e, fill[e]]; fill[e] += 1; slot_token[j] = t; pos[r, t] = j
    g = np.random.uniform(0.2, 0.8, T)
    w = [pack_weight(m, "e2m1") for m in n((E, K, N)) / np.sqrt(K) / s[None]]
    r = mx_kscale(M)[:, None]
    return {
        "uT": (n((M, T)) * r).astype(np.float32),
        "wu": (n((M, K)) / np.sqrt(M) / r * s.T).astype(np.float32),
        "w_words": np.stack([m[0] for m in w]),
        "w_scales": np.stack([m[1] for m in w]),
        "gate": np.stack([np.tile(g, (N, 1)), np.tile(1.0 - g, (N, 1))]).astype(np.float32),
        "offs": striped(slot_token),
        "pos1": striped(pos[0]),
        "pos2": striped(pos[1]),
    }


def reference(uT, wu, w_words, w_scales, gate, offs, pos1, pos2):
    idx = unstriped(offs)
    w = np.stack([unpack_weight(w_words[e], w_scales[e], "e2m1") for e in range(E)])
    x = mxq(f64(wu), 0, "e4m3").T @ mxq(f64(uT), 0, "e4m3")
    xq = mxq(x[:, idx], 0, "e4m3")
    y = by_expert(w, xq)
    return f64(gate[0]) * y[:, unstriped(pos1)] + f64(gate[1]) * y[:, unstriped(pos2)]

@@ -1,0 +1,253 @@
+from contextlib import ExitStack
+
+import concourse.mybir as mybir
+
+F, K, T, E, C, N = 512, 1024, 640, 10, 128, 128
+S = E * C
+FLOPS = 2 * F * K * T + 2 * K * N * S
+
+F32 = mybir.dt.float32
+BF16 = mybir.dt.bfloat16
+I32 = mybir.dt.int32
+U32 = mybir.dt.uint32
+U16 = mybir.dt.uint16
+U8 = mybir.dt.uint8
+FP8X4 = mybir.dt.float8_e4m3fn_x4
+FP4X4 = mybir.dt.float4_e2m1fn_x4
+MULT = mybir.AluOpType.mult
+ADD = mybir.AluOpType.add
+
+P = 128
+PASS = 512
+WINDOW = 704
+TOKEN_PIECES = [(0, 256), (256, 256), (512, 128)]
+SLOT_CHUNKS = [(0, 512), (512, 512), (1024, 256)]
+OUT_PIECES = [(0, 384), (384, 256)]
+
+
+def tile_moe_prv_lin_none_kernel(
+    tc, uT, wu, w_words, w_scales, gate, offs, pos1, pos2, out
+):
+    nc = tc.nc
+    with ExitStack() as ctx:
+        keep = ctx.enter_context(tc.tile_pool(name="keep", bufs=1))
+        psum = ctx.enter_context(tc.psum_pool(name="psum", bufs=1))
+
+        def sb(name, shape, dtype):
+            return keep.tile(shape, dtype, name=name, align_bytes=64)
+
+        offs_sb = keep.tile([P, S // 16], U16, name="offs_sb")
+        pos_sb = [keep.tile([P, T // 16], U16, name="pos_sb%d" % r) for r in range(2)]
+
+        windows = {}
+        for a in range(2):
+            for u in range(2):
+                windows[a, u] = sb("window%d%d" % (a, u), [P, WINDOW], U32)
+                nc.vector.memset(windows[a, u][:, T:WINDOW], 0)
+        ws_sb = sb("ws_sb", [P, 2 * E, N], U8)
+        nc.vector.memset(ws_sb[:].rearrange("p g n -> p (g n)").bitcast(I32), 0)
+
+        wu_view = wu.rearrange("(p j) c -> p j c", j=4)
+        u_view = uT.rearrange("(p j) t -> p j t", j=4)
+        wu_half = [sb("wu_half%d" % h, [P, 4, PASS // 2], F32) for h in range(2)]
+        shared = sb("shared", [P, 5 * PASS], F32)
+        wu_raw1 = shared[:, PASS : 5 * PASS].rearrange("p (j c) -> p j c", j=4)
+        u_raw = [sb("u_raw%d" % i, [P, 4, n], F32) for i, (t0, n) in enumerate(TOKEN_PIECES)]
+        for i, (t0, n) in enumerate(TOKEN_PIECES):
+            nc.sync.dma_start(out=u_raw[i][:], in_=u_view[:, :, t0 : t0 + n])
+            if i == 0:
+                for h in range(2):
+                    nc.sync.dma_start(out=wu_half[h][:], in_=wu_view[:, :, h * 256 : (h + 1) * 256])
+        nc.sync.dma_start(offs_sb[:], offs)
+        nc.sync.dma_start(out=wu_raw1, in_=wu_view[:, :, PASS : 2 * PASS])
+        scale_view = w_scales.rearrange("e a (q r) n -> r q (e a) n", r=4)
+        for r in range(4):
+            nc.sync.dma_start(out=ws_sb[r:P:32, :, :].bitcast(I32), in_=scale_view[r].bitcast(I32))
+        ww_sb = sb("ww_sb", [P, 2 * E, 2 * N], U8)
+        nc.sync.dma_start(
+            out=ww_sb[:].bitcast(I32), in_=w_words.rearrange("e a p b -> p (e a) b").bitcast(I32)
+        )
+        nc.sync.dma_start(pos_sb[0][:], pos1)
+        nc.sync.dma_start(pos_sb[1][:], pos2)
+        gate_sb = sb("gate_sb", [P, 2, T], F32)
+        nc.sync.dma_start(out=gate_sb[:], in_=gate.rearrange("r p t -> p r t"))
+
+        gathered = {}
+        for a in range(2):
+            gathered[a, 0] = sb("gathered%d0" % a, [P, 1024], U32)[:]
+            gathered[a, 1] = shared[:, 0:1024].bitcast(U32)
+        gathered[0, 2] = gathered[1, 2] = sb("gathered2", [P, 512], U32)[:]
+
+        wu_codes, wu_scales, wu_grouped = {}, {}, {}
+
+        def group_wu(a, u, raw, m0, copy):
+            src = raw.rearrange("p j (m u t) -> p u m j t", u=2, t=2)[:, u]
+            dst = wu_grouped[a, u].rearrange("p (t m j) -> p m j t", t=2, j=4)
+            copy(out=dst[:, m0 : m0 + src.shape[1]], in_=src)
+
+        def quantize_wu(a, u):
+            wu_codes[a, u] = sb("wu_codes%d%d" % (a, u), [P, 2 * P], U32)
+            wu_scales[a, u] = sb("wu_scales%d%d" % (a, u), [P, 2 * P], U8)
+            nc.vector.quantize_mx(
+                out=wu_codes[a, u][:].bitcast(FP8X4), scales=wu_scales[a, u][:], in_=wu_grouped[a, u]
+            )
+
+        u_grouped, u_codes, u_scales = {}, {}, {}
+
+        def group_u(i):
+            n = TOKEN_PIECES[i][1]
+            u_grouped[i] = sb("u_grouped%d" % i, [P, 4 * n], BF16)
+            nc.vector.tensor_copy(
+                out=u_grouped[i][:].rearrange("p (c i j) -> p c j i", i=4, j=4),
+                in_=u_raw[i][:].rearrange("p j (c i) -> p c j i", i=4),
+            )
+
+        def quantize_u(i):
+            n = TOKEN_PIECES[i][1]
+            u_codes[i] = sb("u_codes%d" % i, [P, n], U32)
+            u_scales[i] = sb("u_scales%d" % i, [P, n], U8)
+            nc.vector.quantize_mx(out=u_codes[i][:].bitcast(FP8X4), scales=u_scales[i][:], in_=u_grouped[i][:])
+
+        def project(a, u, i, copy):
+            t0, n = TOKEN_PIECES[i]
+            bank = psum.tile([P, 2, n], F32, name="proj", tag="bank", bufs=8)
+            for t in range(2):
+                cols = slice(t * P, (t + 1) * P)
+                nc.tensor.matmul_mx(
+                    out=bank[:, t, :],
+                    lhsT=wu_codes[a, u][:, cols].bitcast(FP8X4),
+                    lhsT_scale=wu_scales[a, u][:, cols],
+                    rhs=u_codes[i][:].bitcast(FP8X4),
+                    rhs_scale=u_scales[i][:],
+                    start=True,
+                    stop=True,
+                )
+            pairs = windows[a, u][:, t0 : t0 + n].bitcast(BF16).rearrange("p (n t) -> p n t", t=2)
+            copy(out=pairs, in_=bank[:].rearrange("p t n -> p n t"))
+
+        def gather(a, u, c, lo=0, hi=None):
+            s0, n = SLOT_CHUNKS[c]
+            hi = n if hi is None else hi
+            nc.vector.tensor_copy(
+                gathered[a, c][:, u * n + lo : u * n + hi],
+                windows[a, u][:].indirect(offs_sb[:, (s0 + lo) // 16 : (s0 + hi) // 16]),
+            )
+
+        woven, x_codes, x_scales = {}, {}, {}
+        for a in range(2):
+            for c, (s0, n) in enumerate(SLOT_CHUNKS):
+                woven[a, c] = sb("woven%d%d" % (a, c), [P, 2 * n], U32)
+                x_codes[a, c] = sb("x_codes%d%d" % (a, c), [P, n], U32)
+                x_scales[a, c] = sb("x_scales%d%d" % (a, c), [P, n], U8)
+
+        def weave(a, c, lo=0, hi=None):
+            hi = SLOT_CHUNKS[c][1] if hi is None else hi
+            nc.scalar.copy(
+                out=woven[a, c][:, 2 * lo : 2 * hi].rearrange("p (n u) -> p n u", u=2),
+                in_=gathered[a, c].rearrange("p (u n) -> p n u", u=2)[:, lo:hi, :],
+            )
+
+        def quantize_x(a, c, lo=0, hi=None):
+            hi = SLOT_CHUNKS[c][1] if hi is None else hi
+            nc.vector.quantize_mx(
+                out=x_codes[a, c][:, lo:hi].bitcast(FP8X4),
+                scales=x_scales[a, c][:, lo:hi],
+                in_=woven[a, c][:, 2 * lo : 2 * hi].bitcast(BF16),
+            )
+
+        y_sb = sb("y_sb", [P, S], F32)
+
+        def expert_pass(c, b, a, dst):
+            e = SLOT_CHUNKS[c][0] // C + b
+            cols = slice(b * C, (b + 1) * C)
+            nc.tensor.matmul_mx(
+                out=dst,
+                lhsT=ww_sb[:, 2 * e + a, :].bitcast(FP4X4),
+                lhsT_scale=ws_sb[:, 2 * e + a, :],
+                rhs=x_codes[a, c][:, cols].bitcast(FP8X4),
+                rhs_scale=x_scales[a, c][:, cols],
+                start=(a == 0),
+                stop=(a == 1),
+            )
+
+        def experts(c):
+            s0, n = SLOT_CHUNKS[c]
+            bank = psum.tile([P, n], F32, name="ybank", tag="bank", bufs=8)
+            for b in range(n // C):
+                for a in range(2):
+                    expert_pass(c, b, a, bank[:, b * C : (b + 1) * C])
+            nc.scalar.copy(out=y_sb[:, s0 : s0 + n], in_=bank[:])
+
+        vcopy, scopy = nc.vector.tensor_copy, nc.scalar.copy
+
+        for u in range(2):
+            wu_grouped[0, u] = sb("wu_grouped%d" % u, [P, 1024], BF16)[:]
+        wu_grouped[1, 0] = gathered[0, 0][:, 512:1024].bitcast(BF16)
+        wu_grouped[1, 1] = sb("wu_grouped3", [P, 1024], BF16)[:]
+        group_u(0)
+        quantize_u(0)
+        for h in range(2):
+            group_wu(0, 0, wu_half[h][:], 64 * h, vcopy)
+            group_wu(0, 1, wu_half[h][:], 64 * h, scopy)
+        quantize_wu(0, 0)
+        project(0, 0, 0, scopy)
+        group_u(1)
+        group_u(2)
+        quantize_u(1)
+        quantize_u(2)
+        project(0, 0, 1, scopy)
+        project(0, 0, 2, vcopy)
+        quantize_wu(0, 1)
+        for i in range(3):
+            project(0, 1, i, scopy)
+        for c in range(3):
+            gather(0, 0, c)
+        for u in range(2):
+            group_wu(1, u, wu_raw1, 0, scopy)
+            quantize_wu(1, u)
+        for c in range(3):
+            gather(0, 1, c)
+        for u in range(2):
+            for i in range(3):
+                project(1, u, i, scopy)
+        for u in range(2):
+            gather(1, u, 0)
+        weave(0, 0)
+        quantize_x(0, 0)
+        weave(0, 1)
+        for u in range(2):
+            gather(1, u, 1)
+        quantize_x(0, 1)
+        for c in range(2):
+            weave(1, c)
+            quantize_x(1, c)
+        weave(0, 2)
+        gather(1, 0, 2)
+        for b in range(2):
+            gather(1, 1, 2, b * C, (b + 1) * C)
+        quantize_x(0, 2)
+        experts(0)
+        last = [psum.tile([P, C], F32, name="last%d" % b, tag="bank", bufs=8) for b in range(2)]
+        for b in range(2):
+            weave(1, 2, b * C, (b + 1) * C)
+            quantize_x(1, 2, b * C, (b + 1) * C)
+        experts(1)
+        for a in range(2):
+            for b in range(2):
+                expert_pass(2, b, a, last[b][:])
+        for b in range(2):
+            vcopy(out=y_sb[:, 1024 + b * C : 1024 + (b + 1) * C], in_=last[b][:])
+
+        parts = [sb("part%d" % r, [P, 384], F32) for r in range(3)]
+        for i, (t0, n) in enumerate(OUT_PIECES):
+            mine = [parts[0][:, 0:n], parts[1][:, 0:n]] if i == 0 else [parts[2][:, 0:n], parts[0][:, 0:n]]
+            for r in range(2):
+                nc.vector.tensor_tensor(
+                    mine[r],
+                    y_sb[:].indirect(pos_sb[r][:, t0 // 16 : (t0 + n) // 16]),
+                    gate_sb[:, r, t0 : t0 + n],
+                    MULT,
+                )
+            total = sb("total%d" % i, [P, n], F32)
+            nc.vector.tensor_tensor(total[:], mine[0], mine[1], ADD)
+            nc.sync.dma_start(out=out[:, t0 : t0 + n], in_=total[:])

@@ -19,7 +19,8 @@ ADD = mybir.AluOpType.add
 
 P = 128
 PASS = 512
-WINDOW = 704
+WIDE = 1728
+NARROW = 704
 TOKEN_PIECES = [(0, 256), (256, 256), (512, 128)]
 SLOT_CHUNKS = [(0, 512), (512, 512), (1024, 256)]
 OUT_PIECES = [(0, 384), (384, 256)]
@@ -39,19 +40,19 @@ def tile_moe_prv_lin_none_kernel(
         offs_sb = keep.tile([P, S // 16], U16, name="offs_sb")
         pos_sb = [keep.tile([P, T // 16], U16, name="pos_sb%d" % r) for r in range(2)]
 
-        windows = {}
-        for a in range(2):
-            for u in range(2):
-                windows[a, u] = sb("window%d%d" % (a, u), [P, WINDOW], U32)
-                nc.vector.memset(windows[a, u][:, T:WINDOW], 0)
+        table = sb("table", [P, 3 * T + WIDE], U32)
+        nc.vector.memset(table[:, 4 * T : 3 * T + WIDE], 0)
+
+        def table_start(a, u):
+            return (3 - 2 * a - u) * T
+
         ws_sb = sb("ws_sb", [P, 2 * E, N], U8)
         nc.vector.memset(ws_sb[:].rearrange("p g n -> p (g n)").bitcast(I32), 0)
 
         wu_view = wu.rearrange("(p j) c -> p j c", j=4)
         u_view = uT.rearrange("(p j) t -> p j t", j=4)
         wu_half = [sb("wu_half%d" % h, [P, 4, PASS // 2], F32) for h in range(2)]
-        shared = sb("shared", [P, 5 * PASS], F32)
-        wu_raw1 = shared[:, PASS : 5 * PASS].rearrange("p (j c) -> p j c", j=4)
+        wu_raw1 = sb("wu_raw1", [P, 4, PASS], F32)[:]
         u_raw = [sb("u_raw%d" % i, [P, 4, n], F32) for i, (t0, n) in enumerate(TOKEN_PIECES)]
         for i, (t0, n) in enumerate(TOKEN_PIECES):
             nc.sync.dma_start(out=u_raw[i][:], in_=u_view[:, :, t0 : t0 + n])
@@ -72,11 +73,13 @@ def tile_moe_prv_lin_none_kernel(
         gate_sb = sb("gate_sb", [P, 2, T], F32)
         nc.sync.dma_start(out=gate_sb[:], in_=gate.rearrange("r p t -> p r t"))
 
-        gathered = {}
-        for a in range(2):
-            gathered[a, 0] = sb("gathered%d0" % a, [P, 1024], U32)[:]
-            gathered[a, 1] = shared[:, 0:1024].bitcast(U32)
-        gathered[0, 2] = gathered[1, 2] = sb("gathered2", [P, 512], U32)[:]
+        arena = keep.tile([P, 3 * S], U32, name="arena", tag="arena", align_bytes=64)
+
+        def gathered(a, c):
+            s0, n = SLOT_CHUNKS[c]
+            first = (1 - a) * S + s0
+            step = S - PASS if (a, c) == (1, 2) else S
+            return first, step
 
         wu_codes, wu_scales, wu_grouped = {}, {}, {}
 
@@ -94,19 +97,21 @@ def tile_moe_prv_lin_none_kernel(
 
         u_grouped, u_codes, u_scales = {}, {}, {}
 
-        def group_u(i):
-            n = TOKEN_PIECES[i][1]
-            u_grouped[i] = sb("u_grouped%d" % i, [P, 4 * n], BF16)
-            nc.vector.tensor_copy(
-                out=u_grouped[i][:].rearrange("p (c i j) -> p c j i", i=4, j=4),
-                in_=u_raw[i][:].rearrange("p j (c i) -> p c j i", i=4),
+        for i in range(2):
+            u_grouped[i] = sb("u_grouped%d" % i, [P, 1024], BF16)[:]
+        u_grouped[2] = u_raw[1][:, 3, :].bitcast(BF16)
+
+        def group_u(i, lo, hi, copy):
+            copy(
+                out=u_grouped[i][:, 4 * lo : 4 * hi].rearrange("p (c i j) -> p c j i", i=4, j=4),
+                in_=u_raw[i][:, :, lo:hi].rearrange("p j (c i) -> p c j i", i=4),
             )
 
         def quantize_u(i):
             n = TOKEN_PIECES[i][1]
             u_codes[i] = sb("u_codes%d" % i, [P, n], U32)
             u_scales[i] = sb("u_scales%d" % i, [P, n], U8)
-            nc.vector.quantize_mx(out=u_codes[i][:].bitcast(FP8X4), scales=u_scales[i][:], in_=u_grouped[i][:])
+            nc.vector.quantize_mx(out=u_codes[i][:].bitcast(FP8X4), scales=u_scales[i][:], in_=u_grouped[i])
 
         def project(a, u, i, copy):
             t0, n = TOKEN_PIECES[i]
@@ -122,15 +127,15 @@ def tile_moe_prv_lin_none_kernel(
                     start=True,
                     stop=True,
                 )
-            pairs = windows[a, u][:, t0 : t0 + n].bitcast(BF16).rearrange("p (n t) -> p n t", t=2)
+            w0 = table_start(a, u) + t0
+            pairs = table[:, w0 : w0 + n].bitcast(BF16).rearrange("p (n t) -> p n t", t=2)
             copy(out=pairs, in_=bank[:].rearrange("p t n -> p n t"))
 
-        def gather(a, u, c, lo=0, hi=None):
-            s0, n = SLOT_CHUNKS[c]
-            hi = n if hi is None else hi
+        def gather(a, u, dst, s0, n, width):
+            w0 = table_start(a, u)
             nc.vector.tensor_copy(
-                gathered[a, c][:, u * n + lo : u * n + hi],
-                windows[a, u][:].indirect(offs_sb[:, (s0 + lo) // 16 : (s0 + hi) // 16]),
+                arena[:, dst : dst + n],
+                table[:, w0 : w0 + width].indirect(offs_sb[:, s0 // 16 : (s0 + n) // 16]),
             )
 
         woven, x_codes, x_scales = {}, {}, {}
@@ -142,9 +147,12 @@ def tile_moe_prv_lin_none_kernel(
 
         def weave(a, c, lo=0, hi=None):
             hi = SLOT_CHUNKS[c][1] if hi is None else hi
+            first, step = gathered(a, c)
+            base = (1 - a) * S if step == S else first
+            both = arena[:, base : base + 2 * step].rearrange("p (u n) -> p n u", u=2)
             nc.scalar.copy(
                 out=woven[a, c][:, 2 * lo : 2 * hi].rearrange("p (n u) -> p n u", u=2),
-                in_=gathered[a, c].rearrange("p (u n) -> p n u", u=2)[:, lo:hi, :],
+                in_=both[:, first - base + lo : first - base + hi, :],
             )
 
         def quantize_x(a, c, lo=0, hi=None):
@@ -155,7 +163,6 @@ def tile_moe_prv_lin_none_kernel(
                 in_=woven[a, c][:, 2 * lo : 2 * hi].bitcast(BF16),
             )
 
-        y_sb = sb("y_sb", [P, S], F32)
 
         def expert_pass(c, b, a, dst):
             e = SLOT_CHUNKS[c][0] // C + b
@@ -170,73 +177,74 @@ def tile_moe_prv_lin_none_kernel(
                 stop=(a == 1),
             )
 
-        def experts(c):
+        def experts(c, copy):
             s0, n = SLOT_CHUNKS[c]
             bank = psum.tile([P, n], F32, name="ybank", tag="bank", bufs=8)
             for b in range(n // C):
                 for a in range(2):
                     expert_pass(c, b, a, bank[:, b * C : (b + 1) * C])
-            nc.scalar.copy(out=y_sb[:, s0 : s0 + n], in_=bank[:])
+            return lambda: copy(out=y_sb[:, s0 : s0 + n], in_=bank[:])
 
         vcopy, scopy = nc.vector.tensor_copy, nc.scalar.copy
 
         for u in range(2):
             wu_grouped[0, u] = sb("wu_grouped%d" % u, [P, 1024], BF16)[:]
-        wu_grouped[1, 0] = gathered[0, 0][:, 512:1024].bitcast(BF16)
+        wu_grouped[1, 0] = arena[:, 2 * S : 2 * S + 512].bitcast(BF16)
         wu_grouped[1, 1] = sb("wu_grouped3", [P, 1024], BF16)[:]
-        group_u(0)
+        group_u(0, 0, 256, vcopy)
         quantize_u(0)
         for h in range(2):
             group_wu(0, 0, wu_half[h][:], 64 * h, vcopy)
             group_wu(0, 1, wu_half[h][:], 64 * h, scopy)
         quantize_wu(0, 0)
+        group_u(1, 0, 128, vcopy)
+        group_u(1, 128, 256, scopy)
         project(0, 0, 0, scopy)
-        group_u(1)
-        group_u(2)
         quantize_u(1)
+        group_u(2, 0, 128, vcopy)
         quantize_u(2)
         project(0, 0, 1, scopy)
         project(0, 0, 2, vcopy)
         quantize_wu(0, 1)
         for i in range(3):
             project(0, 1, i, scopy)
-        for c in range(3):
-            gather(0, 0, c)
+        gather(0, 0, S, 0, S, WIDE)
         for u in range(2):
             group_wu(1, u, wu_raw1, 0, scopy)
             quantize_wu(1, u)
-        for c in range(3):
-            gather(0, 1, c)
-        for u in range(2):
-            for i in range(3):
-                project(1, u, i, scopy)
-        for u in range(2):
-            gather(1, u, 0)
+        gather(0, 1, 2 * S, 0, S, WIDE)
+        for i in range(3):
+            project(1, 0, i, scopy)
+        gather(1, 0, 0, 0, S, WIDE)
         weave(0, 0)
         quantize_x(0, 0)
+        for i in range(3):
+            project(1, 1, i, scopy)
+        gather(1, 1, S, 0, 512, NARROW)
         weave(0, 1)
-        for u in range(2):
-            gather(1, u, 1)
+        gather(1, 1, S + 512, 512, 512, NARROW)
         quantize_x(0, 1)
         for c in range(2):
             weave(1, c)
             quantize_x(1, c)
-        weave(0, 2)
-        gather(1, 0, 2)
         for b in range(2):
-            gather(1, 1, 2, b * C, (b + 1) * C)
+            gather(1, 1, S + 512 + b * C, 1024 + b * C, C, NARROW)
+        weave(0, 2)
         quantize_x(0, 2)
-        experts(0)
-        last = [psum.tile([P, C], F32, name="last%d" % b, tag="bank", bufs=8) for b in range(2)]
         for b in range(2):
             weave(1, 2, b * C, (b + 1) * C)
             quantize_x(1, 2, b * C, (b + 1) * C)
-        experts(1)
+        y_sb = keep.tile([P, S], F32, name="y_sb", tag="arena", align_bytes=64)
+        empty0 = experts(0, scopy)
+        empty1 = experts(1, vcopy)
+        last = [psum.tile([P, C], F32, name="last%d" % b, tag="bank", bufs=8) for b in range(2)]
         for a in range(2):
             for b in range(2):
                 expert_pass(2, b, a, last[b][:])
+        empty0()
+        empty1()
         for b in range(2):
-            vcopy(out=y_sb[:, 1024 + b * C : 1024 + (b + 1) * C], in_=last[b][:])
+            scopy(out=y_sb[:, 1024 + b * C : 1024 + (b + 1) * C], in_=last[b][:])
 
         parts = [sb("part%d" % r, [P, 384], F32) for r in range(3)]
         for i, (t0, n) in enumerate(OUT_PIECES):

@@ -51,14 +51,13 @@ def tile_moe_prv_lin_none_kernel(
 
         wu_view = wu.rearrange("(p j) c -> p j c", j=4)
         u_view = uT.rearrange("(p j) t -> p j t", j=4)
-        wu_half = [sb("wu_half%d" % h, [P, 4, PASS // 2], F32) for h in range(2)]
+        wu_raw0 = sb("wu_raw0", [P, 4, PASS], F32)[:]
         wu_raw1 = sb("wu_raw1", [P, 4, PASS], F32)[:]
         u_raw = [sb("u_raw%d" % i, [P, 4, n], F32) for i, (t0, n) in enumerate(TOKEN_PIECES)]
         for i, (t0, n) in enumerate(TOKEN_PIECES):
             nc.sync.dma_start(out=u_raw[i][:], in_=u_view[:, :, t0 : t0 + n])
             if i == 0:
-                for h in range(2):
-                    nc.sync.dma_start(out=wu_half[h][:], in_=wu_view[:, :, h * 256 : (h + 1) * 256])
+                nc.sync.dma_start(out=wu_raw0, in_=wu_view[:, :, 0:PASS])
         nc.sync.dma_start(offs_sb[:], offs)
         nc.sync.dma_start(out=wu_raw1, in_=wu_view[:, :, PASS : 2 * PASS])
         scale_view = w_scales.rearrange("e a (q r) n -> r q (e a) n", r=4)
@@ -193,9 +192,8 @@ def tile_moe_prv_lin_none_kernel(
         wu_grouped[1, 1] = sb("wu_grouped3", [P, 1024], BF16)[:]
         group_u(0, 0, 256, vcopy)
         quantize_u(0)
-        for h in range(2):
-            group_wu(0, 0, wu_half[h][:], 64 * h, vcopy)
-            group_wu(0, 1, wu_half[h][:], 64 * h, scopy)
+        group_wu(0, 0, wu_raw0, 0, vcopy)
+        group_wu(0, 1, wu_raw0, 0, scopy)
         quantize_wu(0, 0)
         group_u(1, 0, 128, vcopy)
         group_u(1, 128, 256, scopy)
@@ -235,16 +233,22 @@ def tile_moe_prv_lin_none_kernel(
             weave(1, 2, b * C, (b + 1) * C)
             quantize_x(1, 2, b * C, (b + 1) * C)
         y_sb = keep.tile([P, S], F32, name="y_sb", tag="arena", align_bytes=64)
+        alone = {}
+        for c in range(1, 3):
+            for b in range(SLOT_CHUNKS[c][1] // C):
+                alone[c, b] = psum.tile([P, C], F32, name="alone%d%d" % (c, b), tag="bank", bufs=8)
+        for b in range(4):
+            expert_pass(1, b, 0, alone[1, b][:])
         empty0 = experts(0, scopy)
-        empty1 = experts(1, vcopy)
-        last = [psum.tile([P, C], F32, name="last%d" % b, tag="bank", bufs=8) for b in range(2)]
+        for b in range(4):
+            expert_pass(1, b, 1, alone[1, b][:])
         for a in range(2):
             for b in range(2):
-                expert_pass(2, b, a, last[b][:])
+                expert_pass(2, b, a, alone[2, b][:])
         empty0()
-        empty1()
-        for b in range(2):
-            scopy(out=y_sb[:, 1024 + b * C : 1024 + (b + 1) * C], in_=last[b][:])
+        for (c, b), bank in alone.items():
+            s0 = SLOT_CHUNKS[c][0] + b * C
+            (vcopy if c == 1 else scopy)(out=y_sb[:, s0 : s0 + C], in_=bank[:])
 
         parts = [sb("part%d" % r, [P, 384], F32) for r in range(3)]
         for i, (t0, n) in enumerate(OUT_PIECES):

@@ -19,6 +19,8 @@ ADD = mybir.AluOpType.add
 
 P = 128
 PASS = 512
+PER_COLUMN = 16
+BANKS = 8
 WIDE = 1728
 NARROW = 704
 TOKEN_PIECES = [(0, 256), (256, 256), (512, 128)]
@@ -30,6 +32,7 @@ def tile_moe_prv_lin_none_kernel(
     tc, uT, wu, w_words, w_scales, gate, offs, pos1, pos2, out
 ):
     nc = tc.nc
+    on_vector, on_scalar = nc.vector.tensor_copy, nc.scalar.copy
     with ExitStack() as ctx:
         keep = ctx.enter_context(tc.tile_pool(name="keep", bufs=1))
         psum = ctx.enter_context(tc.psum_pool(name="psum", bufs=1))
@@ -37,8 +40,8 @@ def tile_moe_prv_lin_none_kernel(
         def sb(name, shape, dtype):
             return keep.tile(shape, dtype, name=name, align_bytes=64)
 
-        offs_sb = keep.tile([P, S // 16], U16, name="offs_sb")
-        pos_sb = [keep.tile([P, T // 16], U16, name="pos_sb%d" % r) for r in range(2)]
+        offs_sb = keep.tile([P, S // PER_COLUMN], U16, name="offs_sb")
+        pos_sb = [keep.tile([P, T // PER_COLUMN], U16, name="pos_sb%d" % r) for r in range(2)]
 
         table = sb("table", [P, 3 * T + WIDE], U32)
         nc.vector.memset(table[:, 4 * T : 3 * T + WIDE], 0)
@@ -51,15 +54,22 @@ def tile_moe_prv_lin_none_kernel(
 
         wu_view = wu.rearrange("(p j) c -> p j c", j=4)
         u_view = uT.rearrange("(p j) t -> p j t", j=4)
-        wu_raw0 = sb("wu_raw0", [P, 4, PASS], F32)[:]
-        wu_raw1 = sb("wu_raw1", [P, 4, PASS], F32)[:]
+        wu_raw = [sb("wu_raw%d" % a, [P, 4, PASS], F32) for a in range(2)]
         u_raw = [sb("u_raw%d" % i, [P, 4, n], F32) for i, (t0, n) in enumerate(TOKEN_PIECES)]
-        for i, (t0, n) in enumerate(TOKEN_PIECES):
+
+        def load_u(i):
+            t0, n = TOKEN_PIECES[i]
             nc.sync.dma_start(out=u_raw[i][:], in_=u_view[:, :, t0 : t0 + n])
-            if i == 0:
-                nc.sync.dma_start(out=wu_raw0, in_=wu_view[:, :, 0:PASS])
+
+        def load_wu(a):
+            nc.sync.dma_start(out=wu_raw[a][:], in_=wu_view[:, :, a * PASS : (a + 1) * PASS])
+
+        load_u(0)
+        load_wu(0)
+        load_u(1)
+        load_u(2)
         nc.sync.dma_start(offs_sb[:], offs)
-        nc.sync.dma_start(out=wu_raw1, in_=wu_view[:, :, PASS : 2 * PASS])
+        load_wu(1)
         scale_view = w_scales.rearrange("e a (q r) n -> r q (e a) n", r=4)
         for r in range(4):
             nc.sync.dma_start(out=ws_sb[r:P:32, :, :].bitcast(I32), in_=scale_view[r].bitcast(I32))
@@ -72,20 +82,22 @@ def tile_moe_prv_lin_none_kernel(
         gate_sb = sb("gate_sb", [P, 2, T], F32)
         nc.sync.dma_start(out=gate_sb[:], in_=gate.rearrange("r p t -> p r t"))
 
-        arena = keep.tile([P, 3 * S], U32, name="arena", tag="arena", align_bytes=64)
+        picked = keep.tile([P, 3 * S], U32, name="picked", tag="picked", align_bytes=64)
+        middle, last = SLOT_CHUNKS[1][0], SLOT_CHUNKS[2][0]
 
-        def gathered(a, c):
+        def picked_pairs(a, c):
             s0, n = SLOT_CHUNKS[c]
-            first = (1 - a) * S + s0
-            step = S - PASS if (a, c) == (1, 2) else S
-            return first, step
+            if (a, c) == (1, 2):
+                apart = S + middle - last
+                return picked[:, last : last + 2 * apart].rearrange("p (u n) -> p n u", u=2)[:, 0:n, :]
+            start = (1 - a) * S
+            return picked[:, start : start + 2 * S].rearrange("p (u n) -> p n u", u=2)[:, s0 : s0 + n, :]
 
         wu_codes, wu_scales, wu_grouped = {}, {}, {}
 
-        def group_wu(a, u, raw, m0, copy):
-            src = raw.rearrange("p j (m u t) -> p u m j t", u=2, t=2)[:, u]
-            dst = wu_grouped[a, u].rearrange("p (t m j) -> p m j t", t=2, j=4)
-            copy(out=dst[:, m0 : m0 + src.shape[1]], in_=src)
+        def group_wu(a, u, copy):
+            src = wu_raw[a][:].rearrange("p j (m u t) -> p u m j t", u=2, t=2)[:, u]
+            copy(out=wu_grouped[a, u].rearrange("p (t m j) -> p m j t", t=2, j=4), in_=src)
 
         def quantize_wu(a, u):
             wu_codes[a, u] = sb("wu_codes%d%d" % (a, u), [P, 2 * P], U32)
@@ -95,9 +107,8 @@ def tile_moe_prv_lin_none_kernel(
             )
 
         u_grouped, u_codes, u_scales = {}, {}, {}
-
         for i in range(2):
-            u_grouped[i] = sb("u_grouped%d" % i, [P, 1024], BF16)[:]
+            u_grouped[i] = sb("u_grouped%d" % i, [P, 4 * TOKEN_PIECES[i][1]], BF16)[:]
         u_grouped[2] = u_raw[1][:, 3, :].bitcast(BF16)
 
         def group_u(i, lo, hi, copy):
@@ -114,7 +125,7 @@ def tile_moe_prv_lin_none_kernel(
 
         def project(a, u, i, copy):
             t0, n = TOKEN_PIECES[i]
-            bank = psum.tile([P, 2, n], F32, name="proj", tag="bank", bufs=8)
+            bank = psum.tile([P, 2, n], F32, name="proj", tag="bank", bufs=BANKS)
             for t in range(2):
                 cols = slice(t * P, (t + 1) * P)
                 nc.tensor.matmul_mx(
@@ -133,8 +144,8 @@ def tile_moe_prv_lin_none_kernel(
         def gather(a, u, dst, s0, n, width):
             w0 = table_start(a, u)
             nc.vector.tensor_copy(
-                arena[:, dst : dst + n],
-                table[:, w0 : w0 + width].indirect(offs_sb[:, s0 // 16 : (s0 + n) // 16]),
+                picked[:, dst : dst + n],
+                table[:, w0 : w0 + width].indirect(offs_sb[:, s0 // PER_COLUMN : (s0 + n) // PER_COLUMN]),
             )
 
         woven, x_codes, x_scales = {}, {}, {}
@@ -144,24 +155,21 @@ def tile_moe_prv_lin_none_kernel(
                 x_codes[a, c] = sb("x_codes%d%d" % (a, c), [P, n], U32)
                 x_scales[a, c] = sb("x_scales%d%d" % (a, c), [P, n], U8)
 
-        def weave(a, c, lo=0, hi=None):
-            hi = SLOT_CHUNKS[c][1] if hi is None else hi
-            first, step = gathered(a, c)
-            base = (1 - a) * S if step == S else first
-            both = arena[:, base : base + 2 * step].rearrange("p (u n) -> p n u", u=2)
+        def weave(a, c, lo, hi):
             nc.scalar.copy(
                 out=woven[a, c][:, 2 * lo : 2 * hi].rearrange("p (n u) -> p n u", u=2),
-                in_=both[:, first - base + lo : first - base + hi, :],
+                in_=picked_pairs(a, c)[:, lo:hi, :],
             )
 
-        def quantize_x(a, c, lo=0, hi=None):
-            hi = SLOT_CHUNKS[c][1] if hi is None else hi
+        def quantize_x(a, c, lo, hi):
             nc.vector.quantize_mx(
                 out=x_codes[a, c][:, lo:hi].bitcast(FP8X4),
                 scales=x_scales[a, c][:, lo:hi],
                 in_=woven[a, c][:, 2 * lo : 2 * hi].bitcast(BF16),
             )
 
+        def whole(c):
+            return 0, SLOT_CHUNKS[c][1]
 
         def expert_pass(c, b, a, dst):
             e = SLOT_CHUNKS[c][0] // C + b
@@ -176,90 +184,92 @@ def tile_moe_prv_lin_none_kernel(
                 stop=(a == 1),
             )
 
-        def experts(c, copy):
-            s0, n = SLOT_CHUNKS[c]
-            bank = psum.tile([P, n], F32, name="ybank", tag="bank", bufs=8)
-            for b in range(n // C):
-                for a in range(2):
-                    expert_pass(c, b, a, bank[:, b * C : (b + 1) * C])
-            return lambda: copy(out=y_sb[:, s0 : s0 + n], in_=bank[:])
-
-        vcopy, scopy = nc.vector.tensor_copy, nc.scalar.copy
-
         for u in range(2):
-            wu_grouped[0, u] = sb("wu_grouped%d" % u, [P, 1024], BF16)[:]
-        wu_grouped[1, 0] = arena[:, 2 * S : 2 * S + 512].bitcast(BF16)
-        wu_grouped[1, 1] = sb("wu_grouped3", [P, 1024], BF16)[:]
-        group_u(0, 0, 256, vcopy)
+            wu_grouped[0, u] = sb("wu_grouped0%d" % u, [P, 8 * P], BF16)[:]
+        wu_grouped[1, 0] = picked[:, 2 * S : 2 * S + 4 * P].bitcast(BF16)
+        wu_grouped[1, 1] = sb("wu_grouped11", [P, 8 * P], BF16)[:]
+
+        group_u(0, 0, 256, on_vector)
         quantize_u(0)
-        group_wu(0, 0, wu_raw0, 0, vcopy)
-        group_wu(0, 1, wu_raw0, 0, scopy)
+        group_wu(0, 0, on_vector)
+        group_wu(0, 1, on_scalar)
         quantize_wu(0, 0)
-        group_u(1, 0, 128, vcopy)
-        group_u(1, 128, 256, scopy)
-        project(0, 0, 0, scopy)
+        group_u(1, 0, 128, on_vector)
+        group_u(1, 128, 256, on_scalar)
+        project(0, 0, 0, on_scalar)
         quantize_u(1)
-        group_u(2, 0, 128, vcopy)
+        group_u(2, 0, 128, on_vector)
         quantize_u(2)
-        project(0, 0, 1, scopy)
-        project(0, 0, 2, vcopy)
+        project(0, 0, 1, on_vector)
+        project(0, 0, 2, on_scalar)
         quantize_wu(0, 1)
-        for i in range(3):
-            project(0, 1, i, scopy)
+        pieces = range(len(TOKEN_PIECES))
+        for i in pieces:
+            project(0, 1, i, on_scalar)
+
         gather(0, 0, S, 0, S, WIDE)
         for u in range(2):
-            group_wu(1, u, wu_raw1, 0, scopy)
+            group_wu(1, u, on_scalar)
             quantize_wu(1, u)
         gather(0, 1, 2 * S, 0, S, WIDE)
-        for i in range(3):
-            project(1, 0, i, scopy)
+        for i in pieces:
+            project(1, 0, i, on_scalar)
         gather(1, 0, 0, 0, S, WIDE)
-        weave(0, 0)
-        quantize_x(0, 0)
-        for i in range(3):
-            project(1, 1, i, scopy)
-        gather(1, 1, S, 0, 512, NARROW)
-        weave(0, 1)
-        gather(1, 1, S + 512, 512, 512, NARROW)
-        quantize_x(0, 1)
+        weave(0, 0, *whole(0))
+        quantize_x(0, 0, *whole(0))
+        for i in pieces:
+            project(1, 1, i, on_scalar)
+        gather(1, 1, S, *SLOT_CHUNKS[0], NARROW)
+        weave(0, 1, *whole(1))
+        gather(1, 1, S + middle, *SLOT_CHUNKS[1], NARROW)
+        quantize_x(0, 1, *whole(1))
         for c in range(2):
-            weave(1, c)
-            quantize_x(1, c)
+            weave(1, c, *whole(c))
+            quantize_x(1, c, *whole(c))
         for b in range(2):
-            gather(1, 1, S + 512 + b * C, 1024 + b * C, C, NARROW)
-        weave(0, 2)
-        quantize_x(0, 2)
+            gather(1, 1, S + middle + b * C, last + b * C, C, NARROW)
+        weave(0, 2, *whole(2))
+        quantize_x(0, 2, *whole(2))
         for b in range(2):
             weave(1, 2, b * C, (b + 1) * C)
             quantize_x(1, 2, b * C, (b + 1) * C)
-        y_sb = keep.tile([P, S], F32, name="y_sb", tag="arena", align_bytes=64)
+
+        y_sb = keep.tile([P, S], F32, name="y_sb", tag="picked", align_bytes=64)
         alone = {}
         for c in range(1, 3):
             for b in range(SLOT_CHUNKS[c][1] // C):
-                alone[c, b] = psum.tile([P, C], F32, name="alone%d%d" % (c, b), tag="bank", bufs=8)
+                alone[c, b] = psum.tile([P, C], F32, name="alone%d%d" % (c, b), tag="bank", bufs=BANKS)
         for b in range(4):
             expert_pass(1, b, 0, alone[1, b][:])
-        empty0 = experts(0, scopy)
+        shared = psum.tile([P, middle], F32, name="shared", tag="bank", bufs=BANKS)
+        for b in range(4):
+            for a in range(2):
+                expert_pass(0, b, a, shared[:, b * C : (b + 1) * C])
         for b in range(4):
             expert_pass(1, b, 1, alone[1, b][:])
         for a in range(2):
             for b in range(2):
                 expert_pass(2, b, a, alone[2, b][:])
-        empty0()
+        on_scalar(out=y_sb[:, 0:middle], in_=shared[:])
         for (c, b), bank in alone.items():
             s0 = SLOT_CHUNKS[c][0] + b * C
-            (vcopy if c == 1 else scopy)(out=y_sb[:, s0 : s0 + C], in_=bank[:])
+            (on_vector if c == 1 else on_scalar)(out=y_sb[:, s0 : s0 + C], in_=bank[:])
 
-        parts = [sb("part%d" % r, [P, 384], F32) for r in range(3)]
-        for i, (t0, n) in enumerate(OUT_PIECES):
-            mine = [parts[0][:, 0:n], parts[1][:, 0:n]] if i == 0 else [parts[2][:, 0:n], parts[0][:, 0:n]]
-            for r in range(2):
-                nc.vector.tensor_tensor(
-                    mine[r],
-                    y_sb[:].indirect(pos_sb[r][:, t0 // 16 : (t0 + n) // 16]),
-                    gate_sb[:, r, t0 : t0 + n],
-                    MULT,
-                )
-            total = sb("total%d" % i, [P, n], F32)
-            nc.vector.tensor_tensor(total[:], mine[0], mine[1], ADD)
-            nc.sync.dma_start(out=out[:, t0 : t0 + n], in_=total[:])
+        gated = [sb("gated%d" % r, [P, T], F32) for r in range(2)]
+        total = sb("total", [P, T], F32)
+
+        def fetch(r, t0, n):
+            nc.vector.tensor_tensor(
+                gated[r][:, t0 : t0 + n],
+                y_sb[:].indirect(pos_sb[r][:, t0 // PER_COLUMN : (t0 + n) // PER_COLUMN]),
+                gate_sb[:, r, t0 : t0 + n],
+                MULT,
+            )
+
+        fetch(0, 0, T)
+        for t0, n in OUT_PIECES:
+            fetch(1, t0, n)
+        for t0, n in OUT_PIECES:
+            cols = slice(t0, t0 + n)
+            nc.vector.tensor_tensor(total[:, cols], gated[0][:, cols], gated[1][:, cols], ADD)
+            nc.sync.dma_start(out=out[:, cols], in_=total[:, cols])

from contextlib import ExitStack

import concourse.mybir as mybir

F, K, T, E, C, N = 512, 1024, 640, 10, 128, 128
S = E * C
FLOPS = 2 * F * K * T + 2 * K * N * S

F32 = mybir.dt.float32
BF16 = mybir.dt.bfloat16
I32 = mybir.dt.int32
U32 = mybir.dt.uint32
U16 = mybir.dt.uint16
U8 = mybir.dt.uint8
FP8X4 = mybir.dt.float8_e4m3fn_x4
FP4X4 = mybir.dt.float4_e2m1fn_x4
MULT = mybir.AluOpType.mult
ADD = mybir.AluOpType.add

P = 128
PASS = 512
PER_COLUMN = 16
BANKS = 8
WIDE = 1728
NARROW = 704
TOKEN_PIECES = [(0, 256), (256, 256), (512, 128)]
SLOT_CHUNKS = [(0, 512), (512, 512), (1024, 256)]
OUT_PIECES = [(0, 384), (384, 256)]


def tile_moe_prv_lin_none_kernel(
    tc, uT, wu, w_words, w_scales, gate, offs, pos1, pos2, out
):
    nc = tc.nc
    on_vector, on_scalar = nc.vector.tensor_copy, nc.scalar.copy
    with ExitStack() as ctx:
        keep = ctx.enter_context(tc.tile_pool(name="keep", bufs=1))
        psum = ctx.enter_context(tc.psum_pool(name="psum", bufs=1))

        def sb(name, shape, dtype):
            return keep.tile(shape, dtype, name=name, align_bytes=64)

        offs_sb = keep.tile([P, S // PER_COLUMN], U16, name="offs_sb")
        pos_sb = [keep.tile([P, T // PER_COLUMN], U16, name="pos_sb%d" % r) for r in range(2)]

        table = sb("table", [P, 3 * T + WIDE], U32)
        nc.vector.memset(table[:, 4 * T : 3 * T + WIDE], 0)

        def table_start(a, u):
            return (3 - 2 * a - u) * T

        ws_sb = sb("ws_sb", [P, 2 * E, N], U8)
        nc.vector.memset(ws_sb[:].rearrange("p g n -> p (g n)").bitcast(I32), 0)

        wu_view = wu.rearrange("(p j) c -> p j c", j=4)
        u_view = uT.rearrange("(p j) t -> p j t", j=4)
        wu_raw = [sb("wu_raw%d" % a, [P, 4, PASS], F32) for a in range(2)]
        u_raw = [sb("u_raw%d" % i, [P, 4, n], F32) for i, (t0, n) in enumerate(TOKEN_PIECES)]

        def load_u(i):
            t0, n = TOKEN_PIECES[i]
            nc.sync.dma_start(out=u_raw[i][:], in_=u_view[:, :, t0 : t0 + n])

        def load_wu(a):
            nc.sync.dma_start(out=wu_raw[a][:], in_=wu_view[:, :, a * PASS : (a + 1) * PASS])

        load_u(0)
        load_wu(0)
        load_u(1)
        load_u(2)
        nc.sync.dma_start(offs_sb[:], offs)
        load_wu(1)
        scale_view = w_scales.rearrange("e a (q r) n -> r q (e a) n", r=4)
        for r in range(4):
            nc.sync.dma_start(out=ws_sb[r:P:32, :, :].bitcast(I32), in_=scale_view[r].bitcast(I32))
        ww_sb = sb("ww_sb", [P, 2 * E, 2 * N], U8)
        nc.sync.dma_start(
            out=ww_sb[:].bitcast(I32), in_=w_words.rearrange("e a p b -> p (e a) b").bitcast(I32)
        )
        nc.sync.dma_start(pos_sb[0][:], pos1)
        nc.sync.dma_start(pos_sb[1][:], pos2)
        gate_sb = sb("gate_sb", [P, 2, T], F32)
        nc.sync.dma_start(out=gate_sb[:], in_=gate.rearrange("r p t -> p r t"))

        picked = keep.tile([P, 3 * S], U32, name="picked", tag="picked", align_bytes=64)
        middle, last = SLOT_CHUNKS[1][0], SLOT_CHUNKS[2][0]

        def picked_pairs(a, c):
            s0, n = SLOT_CHUNKS[c]
            if (a, c) == (1, 2):
                apart = S + middle - last
                return picked[:, last : last + 2 * apart].rearrange("p (u n) -> p n u", u=2)[:, 0:n, :]
            start = (1 - a) * S
            return picked[:, start : start + 2 * S].rearrange("p (u n) -> p n u", u=2)[:, s0 : s0 + n, :]

        wu_codes, wu_scales, wu_grouped = {}, {}, {}

        def group_wu(a, u, copy):
            src = wu_raw[a][:].rearrange("p j (m u t) -> p u m j t", u=2, t=2)[:, u]
            copy(out=wu_grouped[a, u].rearrange("p (t m j) -> p m j t", t=2, j=4), in_=src)

        def quantize_wu(a, u):
            wu_codes[a, u] = sb("wu_codes%d%d" % (a, u), [P, 2 * P], U32)
            wu_scales[a, u] = sb("wu_scales%d%d" % (a, u), [P, 2 * P], U8)
            nc.vector.quantize_mx(
                out=wu_codes[a, u][:].bitcast(FP8X4), scales=wu_scales[a, u][:], in_=wu_grouped[a, u]
            )

        u_grouped, u_codes, u_scales = {}, {}, {}
        for i in range(2):
            u_grouped[i] = sb("u_grouped%d" % i, [P, 4 * TOKEN_PIECES[i][1]], BF16)[:]
        u_grouped[2] = u_raw[1][:, 3, :].bitcast(BF16)

        def group_u(i, lo, hi, copy):
            copy(
                out=u_grouped[i][:, 4 * lo : 4 * hi].rearrange("p (c i j) -> p c j i", i=4, j=4),
                in_=u_raw[i][:, :, lo:hi].rearrange("p j (c i) -> p c j i", i=4),
            )

        def quantize_u(i):
            n = TOKEN_PIECES[i][1]
            u_codes[i] = sb("u_codes%d" % i, [P, n], U32)
            u_scales[i] = sb("u_scales%d" % i, [P, n], U8)
            nc.vector.quantize_mx(out=u_codes[i][:].bitcast(FP8X4), scales=u_scales[i][:], in_=u_grouped[i])

        def project(a, u, i, copy):
            t0, n = TOKEN_PIECES[i]
            bank = psum.tile([P, 2, n], F32, name="proj", tag="bank", bufs=BANKS)
            for t in range(2):
                cols = slice(t * P, (t + 1) * P)
                nc.tensor.matmul_mx(
                    out=bank[:, t, :],
                    lhsT=wu_codes[a, u][:, cols].bitcast(FP8X4),
                    lhsT_scale=wu_scales[a, u][:, cols],
                    rhs=u_codes[i][:].bitcast(FP8X4),
                    rhs_scale=u_scales[i][:],
                    start=True,
                    stop=True,
                )
            w0 = table_start(a, u) + t0
            pairs = table[:, w0 : w0 + n].bitcast(BF16).rearrange("p (n t) -> p n t", t=2)
            copy(out=pairs, in_=bank[:].rearrange("p t n -> p n t"))

        def gather(a, u, dst, s0, n, width):
            w0 = table_start(a, u)
            nc.vector.tensor_copy(
                picked[:, dst : dst + n],
                table[:, w0 : w0 + width].indirect(offs_sb[:, s0 // PER_COLUMN : (s0 + n) // PER_COLUMN]),
            )

        woven, x_codes, x_scales = {}, {}, {}
        for a in range(2):
            for c, (s0, n) in enumerate(SLOT_CHUNKS):
                woven[a, c] = sb("woven%d%d" % (a, c), [P, 2 * n], U32)
                x_codes[a, c] = sb("x_codes%d%d" % (a, c), [P, n], U32)
                x_scales[a, c] = sb("x_scales%d%d" % (a, c), [P, n], U8)

        def weave(a, c, lo, hi):
            nc.scalar.copy(
                out=woven[a, c][:, 2 * lo : 2 * hi].rearrange("p (n u) -> p n u", u=2),
                in_=picked_pairs(a, c)[:, lo:hi, :],
            )

        def quantize_x(a, c, lo, hi):
            nc.vector.quantize_mx(
                out=x_codes[a, c][:, lo:hi].bitcast(FP8X4),
                scales=x_scales[a, c][:, lo:hi],
                in_=woven[a, c][:, 2 * lo : 2 * hi].bitcast(BF16),
            )

        def whole(c):
            return 0, SLOT_CHUNKS[c][1]

        def expert_pass(c, b, a, dst):
            e = SLOT_CHUNKS[c][0] // C + b
            cols = slice(b * C, (b + 1) * C)
            nc.tensor.matmul_mx(
                out=dst,
                lhsT=ww_sb[:, 2 * e + a, :].bitcast(FP4X4),
                lhsT_scale=ws_sb[:, 2 * e + a, :],
                rhs=x_codes[a, c][:, cols].bitcast(FP8X4),
                rhs_scale=x_scales[a, c][:, cols],
                start=(a == 0),
                stop=(a == 1),
            )

        for u in range(2):
            wu_grouped[0, u] = sb("wu_grouped0%d" % u, [P, 8 * P], BF16)[:]
        wu_grouped[1, 0] = picked[:, 2 * S : 2 * S + 4 * P].bitcast(BF16)
        wu_grouped[1, 1] = sb("wu_grouped11", [P, 8 * P], BF16)[:]

        group_u(0, 0, 256, on_vector)
        quantize_u(0)
        group_wu(0, 0, on_vector)
        group_wu(0, 1, on_scalar)
        quantize_wu(0, 0)
        group_u(1, 0, 128, on_vector)
        group_u(1, 128, 256, on_scalar)
        project(0, 0, 0, on_scalar)
        quantize_u(1)
        group_u(2, 0, 128, on_vector)
        quantize_u(2)
        project(0, 0, 1, on_vector)
        project(0, 0, 2, on_scalar)
        quantize_wu(0, 1)
        pieces = range(len(TOKEN_PIECES))
        for i in pieces:
            project(0, 1, i, on_scalar)

        gather(0, 0, S, 0, S, WIDE)
        for u in range(2):
            group_wu(1, u, on_scalar)
            quantize_wu(1, u)
        gather(0, 1, 2 * S, 0, S, WIDE)
        for i in pieces:
            project(1, 0, i, on_scalar)
        gather(1, 0, 0, 0, S, WIDE)
        weave(0, 0, *whole(0))
        quantize_x(0, 0, *whole(0))
        for i in pieces:
            project(1, 1, i, on_scalar)
        gather(1, 1, S, *SLOT_CHUNKS[0], NARROW)
        weave(0, 1, *whole(1))
        gather(1, 1, S + middle, *SLOT_CHUNKS[1], NARROW)
        quantize_x(0, 1, *whole(1))
        for c in range(2):
            weave(1, c, *whole(c))
            quantize_x(1, c, *whole(c))
        for b in range(2):
            gather(1, 1, S + middle + b * C, last + b * C, C, NARROW)
        weave(0, 2, *whole(2))
        quantize_x(0, 2, *whole(2))
        for b in range(2):
            weave(1, 2, b * C, (b + 1) * C)
            quantize_x(1, 2, b * C, (b + 1) * C)

        y_sb = keep.tile([P, S], F32, name="y_sb", tag="picked", align_bytes=64)
        alone = {}
        for c in range(1, 3):
            for b in range(SLOT_CHUNKS[c][1] // C):
                alone[c, b] = psum.tile([P, C], F32, name="alone%d%d" % (c, b), tag="bank", bufs=BANKS)
        for b in range(4):
            expert_pass(1, b, 0, alone[1, b][:])
        shared = psum.tile([P, middle], F32, name="shared", tag="bank", bufs=BANKS)
        for b in range(4):
            for a in range(2):
                expert_pass(0, b, a, shared[:, b * C : (b + 1) * C])
        for b in range(4):
            expert_pass(1, b, 1, alone[1, b][:])
        for a in range(2):
            for b in range(2):
                expert_pass(2, b, a, alone[2, b][:])
        on_scalar(out=y_sb[:, 0:middle], in_=shared[:])
        for (c, b), bank in alone.items():
            s0 = SLOT_CHUNKS[c][0] + b * C
            (on_vector if c == 1 else on_scalar)(out=y_sb[:, s0 : s0 + C], in_=bank[:])

        gated = [sb("gated%d" % r, [P, T], F32) for r in range(2)]
        total = sb("total", [P, T], F32)

        def fetch(r, t0, n):
            nc.vector.tensor_tensor(
                gated[r][:, t0 : t0 + n],
                y_sb[:].indirect(pos_sb[r][:, t0 // PER_COLUMN : (t0 + n) // PER_COLUMN]),
                gate_sb[:, r, t0 : t0 + n],
                MULT,
            )

        fetch(0, 0, T)
        for t0, n in OUT_PIECES:
            fetch(1, t0, n)
        for t0, n in OUT_PIECES:
            cols = slice(t0, t0 + n)
            nc.vector.tensor_tensor(total[:, cols], gated[0][:, cols], gated[1][:, cols], ADD)
            nc.sync.dma_start(out=out[:, cols], in_=total[:, cols])
